import numpy as np
import ml_dtypes


def mxq(x, axis, fmt="e4m3"):
    dtype, down = {"e4m3": (ml_dtypes.float8_e4m3fn, 7), "e5m2": (ml_dtypes.float8_e5m2, 14)}[fmt]
    v = np.moveaxis(np.asarray(x, np.float32).astype(ml_dtypes.bfloat16).astype(np.float64), axis, -1)
    blocks = v.reshape(v.shape[:-1] + (-1, 32))
    amax = np.abs(blocks).max(-1, keepdims=True)
    byte = np.maximum(np.where(amax > 0, np.frexp(amax)[1] - 1 + 127, 0) - down, 1)
    scale = np.exp2(byte - 127.0)
    codes = (blocks / scale).astype(np.float32).astype(dtype).astype(np.float64)
    return np.moveaxis((codes * scale).reshape(v.shape), -1, axis)


WIDE = False


def mx_kscale(k):
    if not WIDE:
        return np.ones(k)
    levels = np.array([30, -30])
    if k % 512:
        return np.exp2(np.random.permutation(np.resize(levels, k // 32))).repeat(32)
    a = np.empty((k // 512, 16))
    for p in range(k // 512):
        a[p, :8] = np.random.permutation(np.resize(levels, 8))
        for g in range(8):
            far = levels[np.abs(levels - a[p, g]) >= 10]
            a[p, g + 8] = far[np.random.randint(len(far))]
    return np.exp2(a.ravel()).repeat(32)


def f64(x):
    return np.asarray(x).astype(np.float64)


def striped(idx):
    return np.tile(np.asarray(idx).reshape(-1, 16).T, (8, 1)).astype(np.uint16)


def unstriped(offs):
    return offs[:16].T.reshape(-1).astype(np.int64)


E2M1 = np.array([0.0, 0.5, 1.0, 1.5, 2.0, 3.0, 4.0, 6.0, -0.0, -0.5, -1.0, -1.5, -2.0, -3.0, -4.0, -6.0])


def pack_weight(w, fmt):
    k, n = w.shape
    w = f64(np.asarray(w, np.float32).astype(ml_dtypes.bfloat16)).reshape(k // 32, 32, n)
    amax = np.abs(w).max(1)
    if fmt in ("e4m3", "e5m2"):
        byte = np.frexp(amax)[1] - 1 + 127 - (7 if fmt == "e4m3" else 14)
    else:
        mant, ex = np.frexp(amax / 6.0)
        byte = np.where(mant > 0.5, ex, ex - 1) + 127
    byte = np.clip(np.where(amax > 0, byte, 1), 1, 254)
    scaled = (w * np.exp2(127.0 - byte)[:, None, :]).reshape(k, n).astype(np.float32)
    by_word = np.ascontiguousarray(scaled.reshape(k // 512, 128, 4, n).transpose(0, 1, 3, 2))
    if fmt in ("e4m3", "e5m2"):
        words = by_word.astype(ml_dtypes.float8_e4m3fn if fmt == "e4m3" else ml_dtypes.float8_e5m2).view(np.uint8)
    else:
        c = by_word.astype(ml_dtypes.float4_e2m1fn).view(np.uint8) & 0xF
        words = (c[..., 0::2] | (c[..., 1::2] << 4)).reshape(k // 512, 128, 2 * n)
    return np.ascontiguousarray(words), np.ascontiguousarray(byte.astype(np.uint8).reshape(k // 512, 16, n))


def unpack_weight(words, scales, fmt):
    g, _, n = scales.shape
    words = np.ascontiguousarray(words).reshape(g, 128, n, -1)
    if fmt in ("e4m3", "e5m2"):
        vals = words.view(ml_dtypes.float8_e4m3fn if fmt == "e4m3" else ml_dtypes.float8_e5m2).astype(np.float64)
    else:
        nib = np.empty((g, 128, n, 4), np.uint8)
        nib[..., 0::2] = words & 0xF
        nib[..., 1::2] = words >> 4
        vals = E2M1[nib]
    vals = vals * np.repeat(np.exp2(scales.astype(np.float64) - 127.0), 8, axis=1)[..., None]
    return vals.transpose(0, 1, 3, 2).reshape(g * 512, n)


K, T, J, R, V, N = 512, 1024, 256, 512, 512, 256


def setup_inputs():
    n = np.random.standard_normal
    idx = np.random.permutation(T)[:J]
    idx2 = np.random.permutation(V)[:J]
    fk = mx_kscale(K)
    fr = mx_kscale(R)
    wp = pack_weight(n((K, R)) * 1 / np.sqrt(K) * fk[:, None] * fr, "e5m2")
    return {
        "xf": (n((K, T))).astype(np.float32),
        "ow": (n((K, J)) * 0.7).astype(np.float32),
        "fk": (np.random.uniform(0.5, 2.0, (K, 1)) / fk[:, None]).astype(np.float32),
        "w_words": wp[0],
        "w_scales": wp[1],
        "tb": (n((R, V)) * 0.7).astype(np.float32),
        "wb": (n((R, N)) * 1 / np.sqrt(R) / fr[:, None]).astype(np.float32),
        "rs": (n((N, J))).astype(np.float32),
        "gm": (np.random.uniform(0.5, 2.0, (N, 1))).astype(np.float32),
        "offs": striped(idx),
        "offs2": striped(idx2),
    }


def reference(xf, ow, fk, w_words, w_scales, tb, wb, rs, gm, offs, offs2):
    idx = unstriped(offs)
    idx2 = unstriped(offs2)
    wu = unpack_weight(w_words, w_scales, "e5m2")
    u = (f64(xf)[:, idx] - f64(ow)) * f64(fk)
    uq = mxq(u, 0, "e4m3")
    a = wu.T @ uq
    hid = np.maximum(a, 0.0) * f64(tb)[:, idx2]
    wbq = mxq(f64(wb), 0, "e5m2")
    hidq = mxq(hid, 0, "e5m2")
    p = wbq.T @ hidq
    y = f64(gm) * p + f64(rs)
    return y

@@ -1,0 +1,164 @@
+from contextlib import ExitStack
+
+import concourse.mybir as mybir
+
+K, T, J, R, V, N = 512, 1024, 256, 512, 512, 256
+FLOPS = 2 * K * R * J + 2 * R * N * J
+
+F32 = mybir.dt.float32
+BF16 = mybir.dt.bfloat16
+I32 = mybir.dt.int32
+U32 = mybir.dt.uint32
+U16 = mybir.dt.uint16
+U8 = mybir.dt.uint8
+E4M3 = mybir.dt.float8_e4m3fn_x4
+E5M2 = mybir.dt.float8_e5m2_x4
+ALU = mybir.AluOpType
+COPY = mybir.ActivationFunctionType.Copy
+
+P = 128
+PACK = 4
+HALF = J // 2
+LIST_COLS = HALF // 16
+SLOTS = [slice(h * HALF, (h + 1) * HALF) for h in range(2)]
+LIST_SLICES = [slice(h * LIST_COLS, (h + 1) * LIST_COLS) for h in range(2)]
+
+
+def tile_list_offsetpicks_timestable_residual_kernel(
+    tc, xf, ow, fk, w_words, w_scales, tb, wb, rs, gm, offs, offs2, out
+):
+    nc = tc.nc
+    with ExitStack() as ctx:
+        keep = ctx.enter_context(tc.tile_pool(name="keep", bufs=1))
+        psum = ctx.enter_context(tc.psum_pool(name="psum", bufs=1))
+
+        tokens = keep.tile([P, J // 16], U16, name="tokens")
+        entries = keep.tile([P, J // 16], U16, name="entries")
+        w_raw = keep.tile([P, R], U32, name="w_raw")
+        ws_raw = keep.tile([P, R], U8, name="ws_raw")
+        ow_sb = keep.tile([P, PACK, J], F32, name="ow_sb")
+        fk_sb = keep.tile([P, PACK], F32, name="fk_sb")
+        gm_sb = keep.tile([P, 2], F32, name="gm_sb")
+        x_sb = [keep.tile([P, T], F32, name="x%d" % t) for t in range(PACK)]
+        tb_first = keep.tile([P, 2, V], F32, name="tb_first")
+        tb_sb = [tb_first[:, t, :] for t in range(2)] + [keep.tile([P, V], F32, name="tb%d" % t)[:] for t in range(2, PACK)]
+        wb_sb = [keep.tile([P, PACK, P], F32, name="wb_sb%d" % s) for s in range(2)]
+        rs_sb = keep.tile([P, 2, J], F32, name="rs_sb")
+
+        nc.vector.memset(ws_raw[:].bitcast(I32), 0)
+        x_planes = xf.rearrange("(p t) c -> t p c", t=PACK)
+        tb_rows = tb.rearrange("(p t) c -> p t c", t=PACK)
+        wb_rows = wb.rearrange("(p t) n -> p t n", t=PACK)
+        nc.sync.dma_start(tokens[:], offs)
+        nc.scalar.dma_start(fk_sb[:], fk.rearrange("(p t) o -> p (t o)", t=PACK))
+        nc.sync.dma_start(ow_sb[:], ow.rearrange("(p t) j -> p t j", t=PACK))
+        nc.sync.dma_start(x_sb[0][:], x_planes[0])
+        for q in range(4):
+            nc.sync.dma_start(
+                ws_raw[32 * q : 32 * q + 4, :].bitcast(I32), w_scales[0, 4 * q : 4 * q + 4, :].bitcast(I32)
+            )
+        for t in range(1, PACK):
+            nc.sync.dma_start(x_sb[t][:], x_planes[t])
+        nc.sync.dma_start(w_raw[:].bitcast(I32), w_words[0].rearrange("p n t -> p (n t)").bitcast(I32))
+        nc.sync.dma_start(entries[:], offs2)
+        nc.sync.dma_start(tb_first[:], tb_rows[:, 0:2, :])
+        for t in range(2, PACK):
+            nc.sync.dma_start(tb_sb[t], tb_rows[:, t, :])
+        for s in range(2):
+            nc.sync.dma_start(wb_sb[s][:], wb_rows[:, :, s * P : (s + 1) * P])
+        nc.sync.dma_start(rs_sb[:], rs.rearrange("(s p) j -> p s j", p=P))
+        with nc.allow_non_contiguous_dma(reason="one factor a partition for each of two row tiles"):
+            nc.sync.dma_start(gm_sb[:], gm.rearrange("(s p) o -> p (s o)", p=P))
+
+        diff = keep.tile([P, PACK, J], F32, name="diff")
+        u_bf = keep.tile([P, J, PACK], BF16, name="u_bf", align_bytes=64)
+        for t in range(PACK - 1):
+            nc.vector.tensor_tensor(diff[:, t, :], x_sb[t][:].indirect(tokens[:]), ow_sb[:, t, :], ALU.subtract)
+            if t < 2:
+                nc.vector.tensor_scalar(u_bf[:, :, t], diff[:, t, :], fk_sb[:, t : t + 1], None, ALU.mult)
+            else:
+                nc.scalar.activation(u_bf[:, :, t], diff[:, t, :], COPY, scale=fk_sb[:, t : t + 1])
+        t = PACK - 1
+        for h in range(2):
+            nc.vector.tensor_tensor(
+                diff[:, t, SLOTS[h]], x_sb[t][:].indirect(tokens[:, LIST_SLICES[h]]), ow_sb[:, t, SLOTS[h]], ALU.subtract
+            )
+            nc.scalar.activation(u_bf[:, SLOTS[h], t], diff[:, t, SLOTS[h]], COPY, scale=fk_sb[:, t : t + 1])
+
+        w_codes = keep.tile([P, PACK, P], U32, name="w_codes", align_bytes=64)
+        w_sc = keep.tile([P, PACK, P], U8, name="w_sc", align_bytes=64)
+        nc.vector.tensor_copy(w_sc[:], ws_raw[:].rearrange("p (m t) -> p t m", t=PACK))
+        nc.vector.tensor_copy(
+            w_codes[:].rearrange("p t (c i) -> p c t i", i=4), w_raw[:].rearrange("p (c i t) -> p c t i", i=4, t=PACK)
+        )
+
+        u_codes = keep.tile([P, J], U32, name="u_codes", align_bytes=64)
+        u_sc = keep.tile([P, J], U8, name="u_sc", align_bytes=64)
+        a_ps = [psum.tile([P, PACK, HALF], F32, name="a%d" % h) for h in range(2)]
+        for h in range(2):
+            nc.vector.quantize_mx(
+                out=u_codes[:, SLOTS[h]].bitcast(E4M3),
+                scales=u_sc[:, SLOTS[h]],
+                in_=u_bf[:, SLOTS[h], :].rearrange("p j t -> p (j t)"),
+            )
+        for h in range(2):
+            for t in range(PACK):
+                nc.tensor.matmul_mx(
+                    out=a_ps[h][:, t, :],
+                    lhsT=w_codes[:, t, :].bitcast(E5M2),
+                    lhsT_scale=w_sc[:, t, :],
+                    rhs=u_codes[:, SLOTS[h]].bitcast(E4M3),
+                    rhs_scale=u_sc[:, SLOTS[h]],
+                    start=True,
+                    stop=True,
+                )
+
+        picked = [keep.tile([P, PACK, HALF], F32, name="picked%d" % h) for h in range(2)]
+        for t in range(PACK):
+            nc.vector.tensor_copy(picked[0][:, t, :], tb_sb[t].indirect(entries[:, LIST_SLICES[0]]))
+            nc.scalar.activation(picked[1][:, t, :], tb_sb[t].indirect(entries[:, LIST_SLICES[1]]), COPY)
+
+        hid_bf = [keep.tile([P, HALF, PACK], BF16, name="hid_bf%d" % h, align_bytes=64) for h in range(2)]
+        hid_codes = keep.tile([P, J], U32, name="hid_codes", align_bytes=64)
+        hid_sc = keep.tile([P, J], U8, name="hid_sc", align_bytes=64)
+        wb_bf = [keep.tile([P, P, PACK], BF16, name="wb_bf%d" % s, align_bytes=64) for s in range(2)]
+        wb_codes = [keep.tile([P, P], U32, name="wb_codes%d" % s, align_bytes=64) for s in range(2)]
+        wb_sc = [keep.tile([P, P], U8, name="wb_sc%d" % s, align_bytes=64) for s in range(2)]
+        for h in range(2):
+            nc.vector.scalar_tensor_tensor(
+                hid_bf[h][:],
+                a_ps[h][:].rearrange("p t j -> p j t"),
+                0.0,
+                picked[h][:].rearrange("p t j -> p j t"),
+                ALU.max,
+                ALU.mult,
+            )
+        for s in range(2):
+            nc.scalar.copy(
+                wb_bf[s][:].rearrange("p (c i) t -> p c t i", i=4), wb_sb[s][:].rearrange("p t (c i) -> p c t i", i=4)
+            )
+        for h in range(2):
+            nc.vector.quantize_mx(
+                out=hid_codes[:, SLOTS[h]].bitcast(E5M2),
+                scales=hid_sc[:, SLOTS[h]],
+                in_=hid_bf[h][:].rearrange("p j t -> p (j t)"),
+            )
+        for s in range(2):
+            nc.vector.quantize_mx(
+                out=wb_codes[s][:].bitcast(E5M2), scales=wb_sc[s][:], in_=wb_bf[s][:].rearrange("p m t -> p (m t)")
+            )
+        for s in range(2):
+            p_ps = psum.tile([P, J], F32, name="p%d" % s)
+            nc.tensor.matmul_mx(
+                out=p_ps[:],
+                lhsT=wb_codes[s][:].bitcast(E5M2),
+                lhsT_scale=wb_sc[s][:],
+                rhs=hid_codes[:].bitcast(E5M2),
+                rhs_scale=hid_sc[:],
+                start=True,
+                stop=True,
+            )
+            y = keep.tile([P, J], F32, name="y%d" % s)
+            nc.vector.scalar_tensor_tensor(y[:], p_ps[:], gm_sb[:, s : s + 1], rs_sb[:, s, :], ALU.mult, ALU.add)
+            queue = nc.sync if s == 0 else nc.scalar
+            queue.dma_start(out[s * P : (s + 1) * P, :], y[:])

@@ -42,13 +42,12 @@ def tile_list_offsetpicks_timestable_residual_kernel(
         x_sb = [keep.tile([P, T], F32, name="x%d" % t) for t in range(PACK)]
         tb_first = keep.tile([P, 2, V], F32, name="tb_first")
         tb_sb = [tb_first[:, t, :] for t in range(2)] + [keep.tile([P, V], F32, name="tb%d" % t)[:] for t in range(2, PACK)]
-        wb_sb = [keep.tile([P, PACK, P], F32, name="wb_sb%d" % s) for s in range(2)]
+        wb_sb = keep.tile([P, PACK, N], F32, name="wb_sb")
         rs_sb = keep.tile([P, 2, J], F32, name="rs_sb")
 
         nc.vector.memset(ws_raw[:].bitcast(I32), 0)
         x_planes = xf.rearrange("(p t) c -> t p c", t=PACK)
         tb_rows = tb.rearrange("(p t) c -> p t c", t=PACK)
-        wb_rows = wb.rearrange("(p t) n -> p t n", t=PACK)
         nc.sync.dma_start(tokens[:], offs)
         nc.scalar.dma_start(fk_sb[:], fk.rearrange("(p t) o -> p (t o)", t=PACK))
         nc.sync.dma_start(ow_sb[:], ow.rearrange("(p t) j -> p t j", t=PACK))
@@ -64,26 +63,22 @@ def tile_list_offsetpicks_timestable_residual_kernel(
         nc.sync.dma_start(tb_first[:], tb_rows[:, 0:2, :])
         for t in range(2, PACK):
             nc.sync.dma_start(tb_sb[t], tb_rows[:, t, :])
-        for s in range(2):
-            nc.sync.dma_start(wb_sb[s][:], wb_rows[:, :, s * P : (s + 1) * P])
-        nc.sync.dma_start(rs_sb[:], rs.rearrange("(s p) j -> p s j", p=P))
+        nc.sync.dma_start(wb_sb[:], wb.rearrange("(p t) n -> p t n", t=PACK))
         with nc.allow_non_contiguous_dma(reason="one factor a partition for each of two row tiles"):
             nc.sync.dma_start(gm_sb[:], gm.rearrange("(s p) o -> p (s o)", p=P))
+        nc.sync.dma_start(rs_sb[:], rs.rearrange("(s p) j -> p s j", p=P))
 
         diff = keep.tile([P, PACK, J], F32, name="diff")
         u_bf = keep.tile([P, J, PACK], BF16, name="u_bf", align_bytes=64)
-        for t in range(PACK - 1):
-            nc.vector.tensor_tensor(diff[:, t, :], x_sb[t][:].indirect(tokens[:]), ow_sb[:, t, :], ALU.subtract)
-            if t < 2:
-                nc.vector.tensor_scalar(u_bf[:, :, t], diff[:, t, :], fk_sb[:, t : t + 1], None, ALU.mult)
-            else:
-                nc.scalar.activation(u_bf[:, :, t], diff[:, t, :], COPY, scale=fk_sb[:, t : t + 1])
-        t = PACK - 1
-        for h in range(2):
-            nc.vector.tensor_tensor(
-                diff[:, t, SLOTS[h]], x_sb[t][:].indirect(tokens[:, LIST_SLICES[h]]), ow_sb[:, t, SLOTS[h]], ALU.subtract
-            )
-            nc.scalar.activation(u_bf[:, SLOTS[h], t], diff[:, t, SLOTS[h]], COPY, scale=fk_sb[:, t : t + 1])
+        for t in range(PACK):
+            for h in range(2):
+                nc.vector.tensor_tensor(
+                    diff[:, t, SLOTS[h]],
+                    x_sb[t][:].indirect(tokens[:, LIST_SLICES[h]]),
+                    ow_sb[:, t, SLOTS[h]],
+                    ALU.subtract,
+                )
+                nc.scalar.activation(u_bf[:, SLOTS[h], t], diff[:, t, SLOTS[h]], COPY, scale=fk_sb[:, t : t + 1])
 
         w_codes = keep.tile([P, PACK, P], U32, name="w_codes", align_bytes=64)
         w_sc = keep.tile([P, PACK, P], U8, name="w_sc", align_bytes=64)
@@ -94,13 +89,13 @@ def tile_list_offsetpicks_timestable_residual_kernel(
 
         u_codes = keep.tile([P, J], U32, name="u_codes", align_bytes=64)
         u_sc = keep.tile([P, J], U8, name="u_sc", align_bytes=64)
-        a_ps = [psum.tile([P, PACK, HALF], F32, name="a%d" % h) for h in range(2)]
         for h in range(2):
             nc.vector.quantize_mx(
                 out=u_codes[:, SLOTS[h]].bitcast(E4M3),
                 scales=u_sc[:, SLOTS[h]],
                 in_=u_bf[:, SLOTS[h], :].rearrange("p j t -> p (j t)"),
             )
+        a_ps = [psum.tile([P, PACK, HALF], F32, name="a%d" % h) for h in range(2)]
         for h in range(2):
             for t in range(PACK):
                 nc.tensor.matmul_mx(
@@ -115,13 +110,15 @@ def tile_list_offsetpicks_timestable_residual_kernel(
 
         picked = [keep.tile([P, PACK, HALF], F32, name="picked%d" % h) for h in range(2)]
         for t in range(PACK):
-            nc.vector.tensor_copy(picked[0][:, t, :], tb_sb[t].indirect(entries[:, LIST_SLICES[0]]))
-            nc.scalar.activation(picked[1][:, t, :], tb_sb[t].indirect(entries[:, LIST_SLICES[1]]), COPY)
+            on_vector = 1 if t == PACK - 1 else 0
+            on_scalar = 1 - on_vector
+            nc.vector.tensor_copy(picked[on_vector][:, t, :], tb_sb[t].indirect(entries[:, LIST_SLICES[on_vector]]))
+            nc.scalar.activation(picked[on_scalar][:, t, :], tb_sb[t].indirect(entries[:, LIST_SLICES[on_scalar]]), COPY)
 
         hid_bf = [keep.tile([P, HALF, PACK], BF16, name="hid_bf%d" % h, align_bytes=64) for h in range(2)]
-        hid_codes = keep.tile([P, J], U32, name="hid_codes", align_bytes=64)
-        hid_sc = keep.tile([P, J], U8, name="hid_sc", align_bytes=64)
-        wb_bf = [keep.tile([P, P, PACK], BF16, name="wb_bf%d" % s, align_bytes=64) for s in range(2)]
+        hid_codes = [keep.tile([P, HALF], U32, name="hid_codes%d" % h, align_bytes=64) for h in range(2)]
+        hid_sc = [keep.tile([P, HALF], U8, name="hid_sc%d" % h, align_bytes=64) for h in range(2)]
+        wb_bf = [keep.tile([P, P, PACK], BF16, name="wb_bf%d" % s, tag="stage%d" % s, align_bytes=64) for s in range(2)]
         wb_codes = [keep.tile([P, P], U32, name="wb_codes%d" % s, align_bytes=64) for s in range(2)]
         wb_sc = [keep.tile([P, P], U8, name="wb_sc%d" % s, align_bytes=64) for s in range(2)]
         for h in range(2):
@@ -135,30 +132,35 @@ def tile_list_offsetpicks_timestable_residual_kernel(
             )
         for s in range(2):
             nc.scalar.copy(
-                wb_bf[s][:].rearrange("p (c i) t -> p c t i", i=4), wb_sb[s][:].rearrange("p t (c i) -> p c t i", i=4)
+                wb_bf[s][:].rearrange("p (c i) t -> p c t i", i=4),
+                wb_sb[:, :, s * P : (s + 1) * P].rearrange("p t (c i) -> p c t i", i=4),
             )
-        for h in range(2):
+
+        def quantize_hid(h):
             nc.vector.quantize_mx(
-                out=hid_codes[:, SLOTS[h]].bitcast(E5M2),
-                scales=hid_sc[:, SLOTS[h]],
-                in_=hid_bf[h][:].rearrange("p j t -> p (j t)"),
+                out=hid_codes[h][:].bitcast(E5M2), scales=hid_sc[h][:], in_=hid_bf[h][:].rearrange("p j t -> p (j t)")
             )
+
         for s in range(2):
+            quantize_hid(s)
             nc.vector.quantize_mx(
                 out=wb_codes[s][:].bitcast(E5M2), scales=wb_sc[s][:], in_=wb_bf[s][:].rearrange("p m t -> p (m t)")
             )
+        y = [keep.tile([P, J], F32, name="y%d" % s, tag="stage%d" % (1 - s), align_bytes=64) for s in range(2)]
         for s in range(2):
-            p_ps = psum.tile([P, J], F32, name="p%d" % s)
-            nc.tensor.matmul_mx(
-                out=p_ps[:],
-                lhsT=wb_codes[s][:].bitcast(E5M2),
-                lhsT_scale=wb_sc[s][:],
-                rhs=hid_codes[:].bitcast(E5M2),
-                rhs_scale=hid_sc[:],
-                start=True,
-                stop=True,
-            )
-            y = keep.tile([P, J], F32, name="y%d" % s)
-            nc.vector.scalar_tensor_tensor(y[:], p_ps[:], gm_sb[:, s : s + 1], rs_sb[:, s, :], ALU.mult, ALU.add)
-            queue = nc.sync if s == 0 else nc.scalar
-            queue.dma_start(out[s * P : (s + 1) * P, :], y[:])
+            for h in range(2):
+                p_ps = psum.tile([P, HALF], F32, name="p%d%d" % (s, h))
+                nc.tensor.matmul_mx(
+                    out=p_ps[:],
+                    lhsT=wb_codes[s][:].bitcast(E5M2),
+                    lhsT_scale=wb_sc[s][:],
+                    rhs=hid_codes[h][:].bitcast(E5M2),
+                    rhs_scale=hid_sc[h][:],
+                    start=True,
+                    stop=True,
+                )
+                nc.vector.scalar_tensor_tensor(
+                    y[s][:, SLOTS[h]], p_ps[:], gm_sb[:, s : s + 1], rs_sb[:, s, SLOTS[h]], ALU.mult, ALU.add
+                )
+        nc.sync.dma_start(out[0:P, :], y[0][:])
+        nc.scalar.dma_start(out[P : 2 * P, :], y[1][:])

@@ -95,11 +95,11 @@ def tile_list_offsetpicks_timestable_residual_kernel(
                 scales=u_sc[:, SLOTS[h]],
                 in_=u_bf[:, SLOTS[h], :].rearrange("p j t -> p (j t)"),
             )
-        a_ps = [psum.tile([P, PACK, HALF], F32, name="a%d" % h) for h in range(2)]
+        a_ps = [[psum.tile([P, 2, HALF], F32, name="a%d%d" % (pair, h)) for h in range(2)] for pair in range(2)]
         for h in range(2):
             for t in range(PACK):
                 nc.tensor.matmul_mx(
-                    out=a_ps[h][:, t, :],
+                    out=a_ps[t // 2][h][:, t % 2, :],
                     lhsT=w_codes[:, t, :].bitcast(E5M2),
                     lhsT_scale=w_sc[:, t, :],
                     rhs=u_codes[:, SLOTS[h]].bitcast(E4M3),
@@ -108,12 +108,15 @@ def tile_list_offsetpicks_timestable_residual_kernel(
                     stop=True,
                 )
 
-        picked = [keep.tile([P, PACK, HALF], F32, name="picked%d" % h) for h in range(2)]
+        picked = [[keep.tile([P, 2, HALF], F32, name="picked%d%d" % (pair, h)) for h in range(2)] for pair in range(2)]
         for t in range(PACK):
-            on_vector = 1 if t == PACK - 1 else 0
-            on_scalar = 1 - on_vector
-            nc.vector.tensor_copy(picked[on_vector][:, t, :], tb_sb[t].indirect(entries[:, LIST_SLICES[on_vector]]))
-            nc.scalar.activation(picked[on_scalar][:, t, :], tb_sb[t].indirect(entries[:, LIST_SLICES[on_scalar]]), COPY)
+            for h in range(2):
+                dst = picked[t // 2][h][:, t % 2, :]
+                src = tb_sb[t].indirect(entries[:, LIST_SLICES[h]])
+                if t < 2 and h == 0:
+                    nc.vector.tensor_copy(dst, src)
+                else:
+                    nc.scalar.activation(dst, src, COPY)
 
         hid_bf = [keep.tile([P, HALF, PACK], BF16, name="hid_bf%d" % h, align_bytes=64) for h in range(2)]
         hid_codes = [keep.tile([P, HALF], U32, name="hid_codes%d" % h, align_bytes=64) for h in range(2)]
@@ -121,15 +124,16 @@ def tile_list_offsetpicks_timestable_residual_kernel(
         wb_bf = [keep.tile([P, P, PACK], BF16, name="wb_bf%d" % s, tag="stage%d" % s, align_bytes=64) for s in range(2)]
         wb_codes = [keep.tile([P, P], U32, name="wb_codes%d" % s, align_bytes=64) for s in range(2)]
         wb_sc = [keep.tile([P, P], U8, name="wb_sc%d" % s, align_bytes=64) for s in range(2)]
-        for h in range(2):
-            nc.vector.scalar_tensor_tensor(
-                hid_bf[h][:],
-                a_ps[h][:].rearrange("p t j -> p j t"),
-                0.0,
-                picked[h][:].rearrange("p t j -> p j t"),
-                ALU.max,
-                ALU.mult,
-            )
+        for pair in range(2):
+            for h in range(2):
+                nc.vector.scalar_tensor_tensor(
+                    hid_bf[h][:, :, 2 * pair : 2 * pair + 2],
+                    a_ps[pair][h][:].rearrange("p e j -> p j e"),
+                    0.0,
+                    picked[pair][h][:].rearrange("p e j -> p j e"),
+                    ALU.max,
+                    ALU.mult,
+                )
         for s in range(2):
             nc.scalar.copy(
                 wb_bf[s][:].rearrange("p (c i) t -> p c t i", i=4),

@@ -43,7 +43,7 @@ def tile_list_offsetpicks_timestable_residual_kernel(
         tb_first = keep.tile([P, 2, V], F32, name="tb_first")
         tb_sb = [tb_first[:, t, :] for t in range(2)] + [keep.tile([P, V], F32, name="tb%d" % t)[:] for t in range(2, PACK)]
         wb_sb = keep.tile([P, PACK, N], F32, name="wb_sb")
-        rs_sb = keep.tile([P, 2, J], F32, name="rs_sb")
+        rs_sb = [keep.tile([P, J], F32, name="rs%d" % s) for s in range(2)]
 
         nc.vector.memset(ws_raw[:].bitcast(I32), 0)
         x_planes = xf.rearrange("(p t) c -> t p c", t=PACK)
@@ -66,7 +66,8 @@ def tile_list_offsetpicks_timestable_residual_kernel(
         nc.sync.dma_start(wb_sb[:], wb.rearrange("(p t) n -> p t n", t=PACK))
         with nc.allow_non_contiguous_dma(reason="one factor a partition for each of two row tiles"):
             nc.sync.dma_start(gm_sb[:], gm.rearrange("(s p) o -> p (s o)", p=P))
-        nc.sync.dma_start(rs_sb[:], rs.rearrange("(s p) j -> p s j", p=P))
+        for s in range(2):
+            nc.sync.dma_start(rs_sb[s][:], rs[s * P : (s + 1) * P, :])
 
         diff = keep.tile([P, PACK, J], F32, name="diff")
         u_bf = keep.tile([P, J, PACK], BF16, name="u_bf", align_bytes=64)
@@ -109,15 +110,6 @@ def tile_list_offsetpicks_timestable_residual_kernel(
                 )
 
         picked = [[keep.tile([P, 2, HALF], F32, name="picked%d%d" % (pair, h)) for h in range(2)] for pair in range(2)]
-        for t in range(PACK):
-            for h in range(2):
-                dst = picked[t // 2][h][:, t % 2, :]
-                src = tb_sb[t].indirect(entries[:, LIST_SLICES[h]])
-                if t < 2 and h == 0:
-                    nc.vector.tensor_copy(dst, src)
-                else:
-                    nc.scalar.activation(dst, src, COPY)
-
         hid_bf = [keep.tile([P, HALF, PACK], BF16, name="hid_bf%d" % h, align_bytes=64) for h in range(2)]
         hid_codes = [keep.tile([P, HALF], U32, name="hid_codes%d" % h, align_bytes=64) for h in range(2)]
         hid_sc = [keep.tile([P, HALF], U8, name="hid_sc%d" % h, align_bytes=64) for h in range(2)]
@@ -125,6 +117,14 @@ def tile_list_offsetpicks_timestable_residual_kernel(
         wb_codes = [keep.tile([P, P], U32, name="wb_codes%d" % s, align_bytes=64) for s in range(2)]
         wb_sc = [keep.tile([P, P], U8, name="wb_sc%d" % s, align_bytes=64) for s in range(2)]
         for pair in range(2):
+            for t in (2 * pair, 2 * pair + 1):
+                for h in range(2):
+                    dst = picked[pair][h][:, t % 2, :]
+                    src = tb_sb[t].indirect(entries[:, LIST_SLICES[h]])
+                    if (t, h) in ((0, 0), (1, 0), (3, 1)):
+                        nc.vector.tensor_copy(dst, src)
+                    else:
+                        nc.scalar.activation(dst, src, COPY)
             for h in range(2):
                 nc.vector.scalar_tensor_tensor(
                     hid_bf[h][:, :, 2 * pair : 2 * pair + 2],
@@ -136,8 +136,8 @@ def tile_list_offsetpicks_timestable_residual_kernel(
                 )
         for s in range(2):
             nc.scalar.copy(
-                wb_bf[s][:].rearrange("p (c i) t -> p c t i", i=4),
-                wb_sb[:, :, s * P : (s + 1) * P].rearrange("p t (c i) -> p c t i", i=4),
+                wb_bf[s][:].rearrange("p (c i) t -> p c t i", i=2),
+                wb_sb[:, :, s * P : (s + 1) * P].rearrange("p t (c i) -> p c t i", i=2),
             )
 
         def quantize_hid(h):
@@ -164,7 +164,7 @@ def tile_list_offsetpicks_timestable_residual_kernel(
                     stop=True,
                 )
                 nc.vector.scalar_tensor_tensor(
-                    y[s][:, SLOTS[h]], p_ps[:], gm_sb[:, s : s + 1], rs_sb[:, s, SLOTS[h]], ALU.mult, ALU.add
+                    y[s][:, SLOTS[h]], p_ps[:], gm_sb[:, s : s + 1], rs_sb[s][:, SLOTS[h]], ALU.mult, ALU.add
                 )
         nc.sync.dma_start(out[0:P, :], y[0][:])
         nc.scalar.dma_start(out[P : 2 * P, :], y[1][:])

from contextlib import ExitStack

import concourse.mybir as mybir

K, T, J, R, V, N = 512, 1024, 256, 512, 512, 256
FLOPS = 2 * K * R * J + 2 * R * N * J

F32 = mybir.dt.float32
BF16 = mybir.dt.bfloat16
I32 = mybir.dt.int32
U32 = mybir.dt.uint32
U16 = mybir.dt.uint16
U8 = mybir.dt.uint8
E4M3 = mybir.dt.float8_e4m3fn_x4
E5M2 = mybir.dt.float8_e5m2_x4
ALU = mybir.AluOpType
COPY = mybir.ActivationFunctionType.Copy

P = 128
PACK = 4
HALF = J // 2
LIST_COLS = HALF // 16
SLOTS = [slice(h * HALF, (h + 1) * HALF) for h in range(2)]
LIST_SLICES = [slice(h * LIST_COLS, (h + 1) * LIST_COLS) for h in range(2)]


def tile_list_offsetpicks_timestable_residual_kernel(
    tc, xf, ow, fk, w_words, w_scales, tb, wb, rs, gm, offs, offs2, out
):
    nc = tc.nc
    with ExitStack() as ctx:
        keep = ctx.enter_context(tc.tile_pool(name="keep", bufs=1))
        psum = ctx.enter_context(tc.psum_pool(name="psum", bufs=1))

        tokens = keep.tile([P, J // 16], U16, name="tokens")
        entries = keep.tile([P, J // 16], U16, name="entries")
        w_raw = keep.tile([P, R], U32, name="w_raw")
        ws_raw = keep.tile([P, R], U8, name="ws_raw")
        ow_sb = keep.tile([P, PACK, J], F32, name="ow_sb")
        fk_sb = keep.tile([P, PACK], F32, name="fk_sb")
        gm_sb = keep.tile([P, 2], F32, name="gm_sb")
        x_sb = [keep.tile([P, T], F32, name="x%d" % t) for t in range(PACK)]
        tb_first = keep.tile([P, 2, V], F32, name="tb_first")
        tb_sb = [tb_first[:, t, :] for t in range(2)] + [keep.tile([P, V], F32, name="tb%d" % t)[:] for t in range(2, PACK)]
        wb_sb = keep.tile([P, PACK, N], F32, name="wb_sb")
        rs_sb = [keep.tile([P, J], F32, name="rs%d" % s) for s in range(2)]

        nc.vector.memset(ws_raw[:].bitcast(I32), 0)
        x_planes = xf.rearrange("(p t) c -> t p c", t=PACK)
        tb_rows = tb.rearrange("(p t) c -> p t c", t=PACK)
        nc.sync.dma_start(tokens[:], offs)
        nc.scalar.dma_start(fk_sb[:], fk.rearrange("(p t) o -> p (t o)", t=PACK))
        nc.sync.dma_start(ow_sb[:], ow.rearrange("(p t) j -> p t j", t=PACK))
        nc.sync.dma_start(x_sb[0][:], x_planes[0])
        for q in range(4):
            nc.sync.dma_start(
                ws_raw[32 * q : 32 * q + 4, :].bitcast(I32), w_scales[0, 4 * q : 4 * q + 4, :].bitcast(I32)
            )
        for t in range(1, PACK):
            nc.sync.dma_start(x_sb[t][:], x_planes[t])
        nc.sync.dma_start(w_raw[:].bitcast(I32), w_words[0].rearrange("p n t -> p (n t)").bitcast(I32))
        nc.sync.dma_start(entries[:], offs2)
        nc.sync.dma_start(tb_first[:], tb_rows[:, 0:2, :])
        for t in range(2, PACK):
            nc.sync.dma_start(tb_sb[t], tb_rows[:, t, :])
        nc.sync.dma_start(wb_sb[:], wb.rearrange("(p t) n -> p t n", t=PACK))
        with nc.allow_non_contiguous_dma(reason="one factor a partition for each of two row tiles"):
            nc.sync.dma_start(gm_sb[:], gm.rearrange("(s p) o -> p (s o)", p=P))
        for s in range(2):
            nc.sync.dma_start(rs_sb[s][:], rs[s * P : (s + 1) * P, :])

        diff = keep.tile([P, PACK, J], F32, name="diff")
        u_bf = keep.tile([P, J, PACK], BF16, name="u_bf", align_bytes=64)
        for t in range(PACK):
            for h in range(2):
                nc.vector.tensor_tensor(
                    diff[:, t, SLOTS[h]],
                    x_sb[t][:].indirect(tokens[:, LIST_SLICES[h]]),
                    ow_sb[:, t, SLOTS[h]],
                    ALU.subtract,
                )
                nc.scalar.activation(u_bf[:, SLOTS[h], t], diff[:, t, SLOTS[h]], COPY, scale=fk_sb[:, t : t + 1])

        w_codes = keep.tile([P, PACK, P], U32, name="w_codes", align_bytes=64)
        w_sc = keep.tile([P, PACK, P], U8, name="w_sc", align_bytes=64)
        nc.vector.tensor_copy(w_sc[:], ws_raw[:].rearrange("p (m t) -> p t m", t=PACK))
        nc.vector.tensor_copy(
            w_codes[:].rearrange("p t (c i) -> p c t i", i=4), w_raw[:].rearrange("p (c i t) -> p c t i", i=4, t=PACK)
        )

        u_codes = keep.tile([P, J], U32, name="u_codes", align_bytes=64)
        u_sc = keep.tile([P, J], U8, name="u_sc", align_bytes=64)
        for h in range(2):
            nc.vector.quantize_mx(
                out=u_codes[:, SLOTS[h]].bitcast(E4M3),
                scales=u_sc[:, SLOTS[h]],
                in_=u_bf[:, SLOTS[h], :].rearrange("p j t -> p (j t)"),
            )
        a_ps = [[psum.tile([P, 2, HALF], F32, name="a%d%d" % (pair, h)) for h in range(2)] for pair in range(2)]
        for h in range(2):
            for t in range(PACK):
                nc.tensor.matmul_mx(
                    out=a_ps[t // 2][h][:, t % 2, :],
                    lhsT=w_codes[:, t, :].bitcast(E5M2),
                    lhsT_scale=w_sc[:, t, :],
                    rhs=u_codes[:, SLOTS[h]].bitcast(E4M3),
                    rhs_scale=u_sc[:, SLOTS[h]],
                    start=True,
                    stop=True,
                )

        picked = [[keep.tile([P, 2, HALF], F32, name="picked%d%d" % (pair, h)) for h in range(2)] for pair in range(2)]
        hid_bf = [keep.tile([P, HALF, PACK], BF16, name="hid_bf%d" % h, align_bytes=64) for h in range(2)]
        hid_codes = [keep.tile([P, HALF], U32, name="hid_codes%d" % h, align_bytes=64) for h in range(2)]
        hid_sc = [keep.tile([P, HALF], U8, name="hid_sc%d" % h, align_bytes=64) for h in range(2)]
        wb_bf = [keep.tile([P, P, PACK], BF16, name="wb_bf%d" % s, tag="stage%d" % s, align_bytes=64) for s in range(2)]
        wb_codes = [keep.tile([P, P], U32, name="wb_codes%d" % s, align_bytes=64) for s in range(2)]
        wb_sc = [keep.tile([P, P], U8, name="wb_sc%d" % s, align_bytes=64) for s in range(2)]
        for pair in range(2):
            for t in (2 * pair, 2 * pair + 1):
                for h in range(2):
                    dst = picked[pair][h][:, t % 2, :]
                    src = tb_sb[t].indirect(entries[:, LIST_SLICES[h]])
                    if (t, h) in ((0, 0), (1, 0), (3, 1)):
                        nc.vector.tensor_copy(dst, src)
                    else:
                        nc.scalar.activation(dst, src, COPY)
            for h in range(2):
                nc.vector.scalar_tensor_tensor(
                    hid_bf[h][:, :, 2 * pair : 2 * pair + 2],
                    a_ps[pair][h][:].rearrange("p e j -> p j e"),
                    0.0,
                    picked[pair][h][:].rearrange("p e j -> p j e"),
                    ALU.max,
                    ALU.mult,
                )
        for s in range(2):
            nc.scalar.copy(
                wb_bf[s][:].rearrange("p (c i) t -> p c t i", i=2),
                wb_sb[:, :, s * P : (s + 1) * P].rearrange("p t (c i) -> p c t i", i=2),
            )

        def quantize_hid(h):
            nc.vector.quantize_mx(
                out=hid_codes[h][:].bitcast(E5M2), scales=hid_sc[h][:], in_=hid_bf[h][:].rearrange("p j t -> p (j t)")
            )

        for s in range(2):
            quantize_hid(s)
            nc.vector.quantize_mx(
                out=wb_codes[s][:].bitcast(E5M2), scales=wb_sc[s][:], in_=wb_bf[s][:].rearrange("p m t -> p (m t)")
            )
        y = [keep.tile([P, J], F32, name="y%d" % s, tag="stage%d" % (1 - s), align_bytes=64) for s in range(2)]
        for s in range(2):
            for h in range(2):
                p_ps = psum.tile([P, HALF], F32, name="p%d%d" % (s, h))
                nc.tensor.matmul_mx(
                    out=p_ps[:],
                    lhsT=wb_codes[s][:].bitcast(E5M2),
                    lhsT_scale=wb_sc[s][:],
                    rhs=hid_codes[h][:].bitcast(E5M2),
                    rhs_scale=hid_sc[h][:],
                    start=True,
                    stop=True,
                )
                nc.vector.scalar_tensor_tensor(
                    y[s][:, SLOTS[h]], p_ps[:], gm_sb[:, s : s + 1], rs_sb[s][:, SLOTS[h]], ALU.mult, ALU.add
                )
        nc.sync.dma_start(out[0:P, :], y[0][:])
        nc.scalar.dma_start(out[P : 2 * P, :], y[1][:])
